import numpy as np
import ml_dtypes


def mxq(x, axis, fmt="e4m3"):
    dtype, down = {"e4m3": (ml_dtypes.float8_e4m3fn, 7), "e5m2": (ml_dtypes.float8_e5m2, 14)}[fmt]
    v = np.moveaxis(np.asarray(x, np.float32).astype(ml_dtypes.bfloat16).astype(np.float64), axis, -1)
    blocks = v.reshape(v.shape[:-1] + (-1, 32))
    amax = np.abs(blocks).max(-1, keepdims=True)
    byte = np.maximum(np.where(amax > 0, np.frexp(amax)[1] - 1 + 127, 0) - down, 1)
    scale = np.exp2(byte - 127.0)
    codes = (blocks / scale).astype(np.float32).astype(dtype).astype(np.float64)
    return np.moveaxis((codes * scale).reshape(v.shape), -1, axis)


WIDE = False


def mx_kscale(k, group=512):
    if not WIDE:
        return np.ones(k)
    levels = np.array([10, -10, 5, -5, 0])
    if group != 512:
        return np.exp2(np.random.permutation(np.resize(levels, k // group))).repeat(group)
    if k % 512:
        return np.exp2(np.random.permutation(np.resize(levels, k // 32))).repeat(32)
    a = np.empty((k // 512, 16))
    for p in range(k // 512):
        a[p, :8] = np.random.permutation(np.resize(levels, 8))
        for g in range(8):
            far = levels[np.abs(levels - a[p, g]) >= 10]
            a[p, g + 8] = far[np.random.randint(len(far))]
    return np.exp2(a.ravel()).repeat(32)


def f64(x):
    return np.asarray(x).astype(np.float64)


E2M1 = np.array([0.0, 0.5, 1.0, 1.5, 2.0, 3.0, 4.0, 6.0, -0.0, -0.5, -1.0, -1.5, -2.0, -3.0, -4.0, -6.0])


def pack_group(w):
    k, n = w.shape
    w = f64(np.asarray(w, np.float32).astype(ml_dtypes.bfloat16)).reshape(k // 32, 32, n)
    amax = np.abs(w).max(1)
    mant, ex = np.frexp(amax / 6.0)
    byte = np.clip(np.where(amax > 0, np.where(mant > 0.5, ex, ex - 1) + 127, 1), 1, 254)
    scaled = (w * np.exp2(127.0 - byte)[:, None, :]).reshape(k, n).astype(np.float32)
    c = np.ascontiguousarray(scaled.reshape(k // 4, 4, n).transpose(0, 2, 1)).astype(ml_dtypes.float4_e2m1fn).view(np.uint8) & 0xF
    return np.ascontiguousarray((c[..., 0::2] | (c[..., 1::2] << 4)).reshape(k // 4, 2 * n)), byte.astype(np.uint8)


def unpack_group(words, scales):
    p, n = words.shape[0], scales.shape[1]
    words = np.ascontiguousarray(words).reshape(p, n, 2)
    nib = np.empty((p, n, 4), np.uint8)
    nib[..., 0::2] = words & 0xF
    nib[..., 1::2] = words >> 4
    return E2M1[nib].transpose(0, 2, 1).reshape(4 * p, n) * np.repeat(np.exp2(scales.astype(np.float64) - 127.0), 32, axis=0)


def silu(v):
    return v / (1.0 + np.exp(-v))


G, D, M, N = 4, 256, 256, 512


def setup_inputs():
    n = np.random.standard_normal
    s = mx_kscale(D, 0)[:, None]
    w_ = [pack_group(w) for w in n((G, D, M)) / np.sqrt(D) / s]
    return {
        "x": (n((G, D, N)) * s).astype(np.float32),
        "w_words": np.stack([w[0] for w in w_]),
        "w_scales": np.stack([w[1] for w in w_]),
        "b": (0.5 * n((G, M, 1))).astype(np.float32),
    }


def reference(x, w_words, w_scales, b):
    xq = mxq(f64(x), 1, "e4m3")
    y = np.stack([unpack_group(w_words[g], w_scales[g]) for g in range(G)]).transpose(0, 2, 1) @ xq
    y = y + f64(b)
    y = silu(y)
    return y

@@ -1,0 +1,107 @@
+from contextlib import ExitStack
+
+import concourse.mybir as mybir
+
+G, D, M, N = 4, 256, 256, 512
+FLOPS = 2 * G * D * M * N
+
+F32 = mybir.dt.float32
+BF16 = mybir.dt.bfloat16
+I32 = mybir.dt.int32
+U32 = mybir.dt.uint32
+U8 = mybir.dt.uint8
+FP8X4 = mybir.dt.float8_e4m3fn_x4
+FP4X4 = mybir.dt.float4_e2m1fn_x4
+SILU = mybir.ActivationFunctionType.Silu
+
+P = 128
+PACK = 4
+ROWS = D // PACK
+SIDE = P // ROWS
+SETS = G // SIDE
+HALVES = M // P
+QUAD = 32
+
+
+def tile_rows_glin_silu_bias_kernel(tc, x, w_words, w_scales, b, out):
+    nc = tc.nc
+    with ExitStack() as ctx:
+        sb = ctx.enter_context(tc.tile_pool(name="sb", bufs=1))
+        ps = ctx.enter_context(tc.psum_pool(name="ps", bufs=1))
+        ctx.enter_context(tc.manual_schedule())
+
+        ws_sb = sb.tile([P, SETS, M], U8, name="ws_sb", align_bytes=64)
+        b_rows = sb.tile([P, G * HALVES, QUAD], F32, name="b_rows", align_bytes=64)
+        b_cols = sb.tile([P, G * HALVES, QUAD], F32, name="b_cols", align_bytes=64)
+        nc.gpsimd.memset(ws_sb[:].bitcast(I32), 0)
+        nc.vector.memset(b_rows[:], 0.0)
+
+        x_v = x.rearrange("(s c) (p u j) n -> s u (c p) j n", c=SIDE, u=2, j=2)
+        w_v = w_words.bitcast(I32).rearrange("(s c) p n -> s (c p) n", c=SIDE)
+        ws_v = w_scales.bitcast(I32).rearrange("(s c) (q r) m -> c q r s m", c=SIDE, r=4)
+        chunks = [slice(0, 256), slice(256, 512)]
+        raw = []
+        w_sb = []
+        for s in range(SETS):
+            raw.append(sb.tile([P, PACK, N], F32, name="raw%d" % s))
+            w_sb.append(sb.tile([P, 2 * M], U8, name="w%d" % s, align_bytes=64))
+
+        def load_x(s):
+            nc.sync.dma_start(out=raw[s][:, 0:2, :], in_=x_v[s, 0])
+            for cols in chunks:
+                nc.sync.dma_start(out=raw[s][:, 2:4, cols], in_=x_v[s, 1][:, :, cols])
+
+        def load_scales(eng, c):
+            for q in range(2):
+                p0 = ROWS * c + QUAD * q
+                eng.dma_start(out=ws_sb[p0 : p0 + 4].bitcast(I32), in_=ws_v[c, q])
+
+        load_x(0)
+        load_scales(nc.gpsimd, 0)
+        load_scales(nc.sync, 1)
+        nc.gpsimd.dma_start(
+            out=b_rows[0:P:QUAD],
+            in_=b.rearrange("g (h q i) o -> q (g h) (i o)", h=HALVES, i=QUAD),
+        )
+        nc.sync.dma_start(out=w_sb[0][:].bitcast(I32), in_=w_v[0])
+        load_x(1)
+        nc.sync.dma_start(out=w_sb[1][:].bitcast(I32), in_=w_v[1])
+
+        for s in range(SETS):
+            grouped = sb.tile([P, N, PACK], BF16, name="grouped%d" % s, align_bytes=64)
+            codes = sb.tile([P, N], U32, name="codes%d" % s, align_bytes=64)
+            scales = sb.tile([P, N], U8, name="scales%d" % s, align_bytes=64)
+            for cols in chunks:
+                nc.vector.tensor_copy(
+                    out=grouped[:, cols, :].rearrange("p (c i) j -> p c j i", i=4),
+                    in_=raw[s][:, :, cols].rearrange("p j (c i) -> p c j i", i=4),
+                )
+            for cols in chunks:
+                nc.vector.quantize_mx(
+                    out=codes[:, cols].bitcast(FP8X4),
+                    scales=scales[:, cols],
+                    in_=grouped[:, cols, :].rearrange("p n j -> p (n j)"),
+                )
+            if s == 0:
+                nc.vector.transpose(
+                    out=b_cols[:].rearrange("p k i -> p (k i)"),
+                    in_=b_rows[:].rearrange("p k i -> p (k i)"),
+                )
+            for h in range(HALVES):
+                for c in range(SIDE):
+                    g = SIDE * s + c
+                    k = HALVES * g + h
+                    rows = slice(ROWS * c, ROWS * (c + 1))
+                    acc = ps.tile([P, N], F32, name="acc%d" % k)
+                    nc.tensor.matmul_mx(
+                        out=acc[:],
+                        lhsT=w_sb[s][rows, 2 * P * h : 2 * P * (h + 1)].bitcast(FP4X4),
+                        lhsT_scale=ws_sb[rows, s, P * h : P * (h + 1)],
+                        rhs=codes[rows, :].bitcast(FP8X4),
+                        rhs_scale=scales[rows, :],
+                        start=True,
+                        stop=True,
+                    )
+                    res = sb.tile([P, N], F32, name="res%d" % k)
+                    nc.scalar.activation(out=res[:], in_=acc[:], func=SILU, bias=b_cols[:, k, 0:1])
+                    nc.sync.dma_start(out=out[g, P * h : P * (h + 1), :], in_=res[:])

@@ -31,41 +31,29 @@ def tile_rows_glin_silu_bias_kernel(tc, x, w_words, w_scales, b, out):
         ctx.enter_context(tc.manual_schedule())
 
         ws_sb = sb.tile([P, SETS, M], U8, name="ws_sb", align_bytes=64)
-        b_rows = sb.tile([P, G * HALVES, QUAD], F32, name="b_rows", align_bytes=64)
-        b_cols = sb.tile([P, G * HALVES, QUAD], F32, name="b_cols", align_bytes=64)
-        nc.gpsimd.memset(ws_sb[:].bitcast(I32), 0)
+        b_rows = sb.tile([P, QUAD], F32, name="b_rows", align_bytes=64)
+        b_cols = sb.tile([P, QUAD], F32, name="b_cols", align_bytes=64)
         nc.vector.memset(b_rows[:], 0.0)
+        nc.vector.memset(ws_sb[:].bitcast(I32), 0)
 
-        x_v = x.rearrange("(s c) (p u j) n -> s u (c p) j n", c=SIDE, u=2, j=2)
-        w_v = w_words.bitcast(I32).rearrange("(s c) p n -> s (c p) n", c=SIDE)
+        x_v = x.rearrange("(s c) (p j) n -> s (c p) j n", c=SIDE, j=PACK)
+        w_v = w_words.bitcast(I32).rearrange("(s c) p n -> (c p) s n", c=SIDE)
         ws_v = w_scales.bitcast(I32).rearrange("(s c) (q r) m -> c q r s m", c=SIDE, r=4)
         chunks = [slice(0, 256), slice(256, 512)]
-        raw = []
-        w_sb = []
-        for s in range(SETS):
-            raw.append(sb.tile([P, PACK, N], F32, name="raw%d" % s))
-            w_sb.append(sb.tile([P, 2 * M], U8, name="w%d" % s, align_bytes=64))
+        raw = [sb.tile([P, PACK, N], F32, name="raw%d" % s) for s in range(SETS)]
+        w_sb = sb.tile([P, SETS, 2 * M], U8, name="w_sb", align_bytes=64)
 
-        def load_x(s):
-            nc.sync.dma_start(out=raw[s][:, 0:2, :], in_=x_v[s, 0])
-            for cols in chunks:
-                nc.sync.dma_start(out=raw[s][:, 2:4, cols], in_=x_v[s, 1][:, :, cols])
-
-        def load_scales(eng, c):
-            for q in range(2):
-                p0 = ROWS * c + QUAD * q
-                eng.dma_start(out=ws_sb[p0 : p0 + 4].bitcast(I32), in_=ws_v[c, q])
-
-        load_x(0)
-        load_scales(nc.gpsimd, 0)
-        load_scales(nc.sync, 1)
-        nc.gpsimd.dma_start(
-            out=b_rows[0:P:QUAD],
+        nc.sync.dma_start(out=raw[0][:], in_=x_v[0])
+        nc.sync.dma_start(
+            out=b_rows[0:P:4, :],
             in_=b.rearrange("g (h q i) o -> q (g h) (i o)", h=HALVES, i=QUAD),
         )
-        nc.sync.dma_start(out=w_sb[0][:].bitcast(I32), in_=w_v[0])
-        load_x(1)
-        nc.sync.dma_start(out=w_sb[1][:].bitcast(I32), in_=w_v[1])
+        for c in range(SIDE):
+            for q in range(2):
+                p0 = ROWS * c + QUAD * q
+                nc.sync.dma_start(out=ws_sb[p0 : p0 + 4].bitcast(I32), in_=ws_v[c, q])
+        nc.sync.dma_start(out=w_sb[:].bitcast(I32), in_=w_v)
+        nc.sync.dma_start(out=raw[1][:], in_=x_v[1])
 
         for s in range(SETS):
             grouped = sb.tile([P, N, PACK], BF16, name="grouped%d" % s, align_bytes=64)
@@ -76,16 +64,13 @@ def tile_rows_glin_silu_bias_kernel(tc, x, w_words, w_scales, b, out):
                     out=grouped[:, cols, :].rearrange("p (c i) j -> p c j i", i=4),
                     in_=raw[s][:, :, cols].rearrange("p j (c i) -> p c j i", i=4),
                 )
+            if s == 0:
+                nc.vector.transpose(out=b_cols[:], in_=b_rows[:])
             for cols in chunks:
                 nc.vector.quantize_mx(
                     out=codes[:, cols].bitcast(FP8X4),
                     scales=scales[:, cols],
                     in_=grouped[:, cols, :].rearrange("p n j -> p (n j)"),
-                )
-            if s == 0:
-                nc.vector.transpose(
-                    out=b_cols[:].rearrange("p k i -> p (k i)"),
-                    in_=b_rows[:].rearrange("p k i -> p (k i)"),
                 )
             for h in range(HALVES):
                 for c in range(SIDE):
@@ -95,7 +80,7 @@ def tile_rows_glin_silu_bias_kernel(tc, x, w_words, w_scales, b, out):
                     acc = ps.tile([P, N], F32, name="acc%d" % k)
                     nc.tensor.matmul_mx(
                         out=acc[:],
-                        lhsT=w_sb[s][rows, 2 * P * h : 2 * P * (h + 1)].bitcast(FP4X4),
+                        lhsT=w_sb[rows, s, 2 * P * h : 2 * P * (h + 1)].bitcast(FP4X4),
                         lhsT_scale=ws_sb[rows, s, P * h : P * (h + 1)],
                         rhs=codes[rows, :].bitcast(FP8X4),
                         rhs_scale=scales[rows, :],
@@ -103,5 +88,5 @@ def tile_rows_glin_silu_bias_kernel(tc, x, w_words, w_scales, b, out):
                         stop=True,
                     )
                     res = sb.tile([P, N], F32, name="res%d" % k)
-                    nc.scalar.activation(out=res[:], in_=acc[:], func=SILU, bias=b_cols[:, k, 0:1])
+                    nc.scalar.activation(out=res[:], in_=acc[:], func=SILU, bias=b_cols[:, 4 * k : 4 * k + 1])
                     nc.sync.dma_start(out=out[g, P * h : P * (h + 1), :], in_=res[:])

@@ -37,11 +37,11 @@ def tile_rows_glin_silu_bias_kernel(tc, x, w_words, w_scales, b, out):
         nc.vector.memset(ws_sb[:].bitcast(I32), 0)
 
         x_v = x.rearrange("(s c) (p j) n -> s (c p) j n", c=SIDE, j=PACK)
-        w_v = w_words.bitcast(I32).rearrange("(s c) p n -> (c p) s n", c=SIDE)
+        w_v = w_words.bitcast(I32).rearrange("(s c) p n -> s (c p) n", c=SIDE)
         ws_v = w_scales.bitcast(I32).rearrange("(s c) (q r) m -> c q r s m", c=SIDE, r=4)
         chunks = [slice(0, 256), slice(256, 512)]
         raw = [sb.tile([P, PACK, N], F32, name="raw%d" % s) for s in range(SETS)]
-        w_sb = sb.tile([P, SETS, 2 * M], U8, name="w_sb", align_bytes=64)
+        w_sb = [sb.tile([P, 2 * M], U8, name="w%d" % s, align_bytes=64) for s in range(SETS)]
 
         nc.sync.dma_start(out=raw[0][:], in_=x_v[0])
         nc.sync.dma_start(
@@ -52,15 +52,24 @@ def tile_rows_glin_silu_bias_kernel(tc, x, w_words, w_scales, b, out):
             for q in range(2):
                 p0 = ROWS * c + QUAD * q
                 nc.sync.dma_start(out=ws_sb[p0 : p0 + 4].bitcast(I32), in_=ws_v[c, q])
-        nc.sync.dma_start(out=w_sb[:].bitcast(I32), in_=w_v)
-        nc.sync.dma_start(out=raw[1][:], in_=x_v[1])
+        nc.sync.dma_start(out=w_sb[0][:].bitcast(I32), in_=w_v[0])
+        flat_raw = raw[1][:].rearrange("p j n -> p (j n)")
+        flat_x = x_v[1].rearrange("p j n -> p (j n)")
+        for run in (slice(0, 2 * N + 256), slice(3 * N, 3 * N + 256)):
+            nc.sync.dma_start(out=flat_raw[:, run], in_=flat_x[:, run])
+        nc.sync.dma_start(out=raw[1][:, 2:4, chunks[1]], in_=x_v[1][:, 2:4, chunks[1]])
+        nc.sync.dma_start(out=w_sb[1][:].bitcast(I32), in_=w_v[1])
 
         for s in range(SETS):
             grouped = sb.tile([P, N, PACK], BF16, name="grouped%d" % s, align_bytes=64)
             codes = sb.tile([P, N], U32, name="codes%d" % s, align_bytes=64)
             scales = sb.tile([P, N], U8, name="scales%d" % s, align_bytes=64)
-            for cols in chunks:
-                nc.vector.tensor_copy(
+            if s == 0:
+                shares = [(nc.scalar.copy, slice(384, 512)), (nc.vector.tensor_copy, slice(0, 256)), (nc.vector.tensor_copy, slice(256, 384))]
+            else:
+                shares = [(nc.vector.tensor_copy, cols) for cols in chunks]
+            for cast, cols in shares:
+                cast(
                     out=grouped[:, cols, :].rearrange("p (c i) j -> p c j i", i=4),
                     in_=raw[s][:, :, cols].rearrange("p j (c i) -> p c j i", i=4),
                 )
@@ -80,7 +89,7 @@ def tile_rows_glin_silu_bias_kernel(tc, x, w_words, w_scales, b, out):
                     acc = ps.tile([P, N], F32, name="acc%d" % k)
                     nc.tensor.matmul_mx(
                         out=acc[:],
-                        lhsT=w_sb[rows, s, 2 * P * h : 2 * P * (h + 1)].bitcast(FP4X4),
+                        lhsT=w_sb[s][rows, 2 * P * h : 2 * P * (h + 1)].bitcast(FP4X4),
                         lhsT_scale=ws_sb[rows, s, P * h : P * (h + 1)],
                         rhs=codes[rows, :].bitcast(FP8X4),
                         rhs_scale=scales[rows, :],

@@ -36,6 +36,10 @@ def tile_rows_glin_silu_bias_kernel(tc, x, w_words, w_scales, b, out):
         nc.vector.memset(b_rows[:], 0.0)
         nc.vector.memset(ws_sb[:].bitcast(I32), 0)
 
+        warm = sb.tile([P, 2], F32, name="warm")
+        nc.vector.memset(warm[:, 0:1], 0.0)
+        nc.scalar.activation(out=warm[:, 1:2], in_=warm[:, 0:1], func=SILU)
+
         x_v = x.rearrange("(s c) (p j) n -> s (c p) j n", c=SIDE, j=PACK)
         w_v = w_words.bitcast(I32).rearrange("(s c) p n -> s (c p) n", c=SIDE)
         ws_v = w_scales.bitcast(I32).rearrange("(s c) (q r) m -> c q r s m", c=SIDE, r=4)
@@ -65,7 +69,7 @@ def tile_rows_glin_silu_bias_kernel(tc, x, w_words, w_scales, b, out):
             codes = sb.tile([P, N], U32, name="codes%d" % s, align_bytes=64)
             scales = sb.tile([P, N], U8, name="scales%d" % s, align_bytes=64)
             if s == 0:
-                shares = [(nc.scalar.copy, slice(384, 512)), (nc.vector.tensor_copy, slice(0, 256)), (nc.vector.tensor_copy, slice(256, 384))]
+                shares = [(nc.scalar.copy, slice(320, 512)), (nc.vector.tensor_copy, slice(0, 256)), (nc.vector.tensor_copy, slice(256, 320))]
             else:
                 shares = [(nc.vector.tensor_copy, cols) for cols in chunks]
             for cast, cols in shares:
@@ -97,5 +101,9 @@ def tile_rows_glin_silu_bias_kernel(tc, x, w_words, w_scales, b, out):
                         stop=True,
                     )
                     res = sb.tile([P, N], F32, name="res%d" % k)
-                    nc.scalar.activation(out=res[:], in_=acc[:], func=SILU, bias=b_cols[:, 4 * k : 4 * k + 1])
-                    nc.sync.dma_start(out=out[g, P * h : P * (h + 1), :], in_=res[:])
+                    parts = chunks if h == 0 and c == 0 else [slice(0, N)]
+                    for cols in parts:
+                        nc.scalar.activation(
+                            out=res[:, cols], in_=acc[:, cols], func=SILU, bias=b_cols[:, 4 * k : 4 * k + 1]
+                        )
+                        nc.sync.dma_start(out=out[g, P * h : P * (h + 1), cols], in_=res[:, cols])

from contextlib import ExitStack

import concourse.mybir as mybir

G, D, M, N = 4, 256, 256, 512
FLOPS = 2 * G * D * M * N

F32 = mybir.dt.float32
BF16 = mybir.dt.bfloat16
I32 = mybir.dt.int32
U32 = mybir.dt.uint32
U8 = mybir.dt.uint8
FP8X4 = mybir.dt.float8_e4m3fn_x4
FP4X4 = mybir.dt.float4_e2m1fn_x4
SILU = mybir.ActivationFunctionType.Silu

P = 128
PACK = 4
ROWS = D // PACK
SIDE = P // ROWS
SETS = G // SIDE
HALVES = M // P
QUAD = 32


def tile_rows_glin_silu_bias_kernel(tc, x, w_words, w_scales, b, out):
    nc = tc.nc
    with ExitStack() as ctx:
        sb = ctx.enter_context(tc.tile_pool(name="sb", bufs=1))
        ps = ctx.enter_context(tc.psum_pool(name="ps", bufs=1))
        ctx.enter_context(tc.manual_schedule())

        ws_sb = sb.tile([P, SETS, M], U8, name="ws_sb", align_bytes=64)
        b_rows = sb.tile([P, QUAD], F32, name="b_rows", align_bytes=64)
        b_cols = sb.tile([P, QUAD], F32, name="b_cols", align_bytes=64)
        nc.vector.memset(b_rows[:], 0.0)
        nc.vector.memset(ws_sb[:].bitcast(I32), 0)

        warm = sb.tile([P, 2], F32, name="warm")
        nc.vector.memset(warm[:, 0:1], 0.0)
        nc.scalar.activation(out=warm[:, 1:2], in_=warm[:, 0:1], func=SILU)

        x_v = x.rearrange("(s c) (p j) n -> s (c p) j n", c=SIDE, j=PACK)
        w_v = w_words.bitcast(I32).rearrange("(s c) p n -> s (c p) n", c=SIDE)
        ws_v = w_scales.bitcast(I32).rearrange("(s c) (q r) m -> c q r s m", c=SIDE, r=4)
        chunks = [slice(0, 256), slice(256, 512)]
        raw = [sb.tile([P, PACK, N], F32, name="raw%d" % s) for s in range(SETS)]
        w_sb = [sb.tile([P, 2 * M], U8, name="w%d" % s, align_bytes=64) for s in range(SETS)]

        nc.sync.dma_start(out=raw[0][:], in_=x_v[0])
        nc.sync.dma_start(
            out=b_rows[0:P:4, :],
            in_=b.rearrange("g (h q i) o -> q (g h) (i o)", h=HALVES, i=QUAD),
        )
        for c in range(SIDE):
            for q in range(2):
                p0 = ROWS * c + QUAD * q
                nc.sync.dma_start(out=ws_sb[p0 : p0 + 4].bitcast(I32), in_=ws_v[c, q])
        nc.sync.dma_start(out=w_sb[0][:].bitcast(I32), in_=w_v[0])
        flat_raw = raw[1][:].rearrange("p j n -> p (j n)")
        flat_x = x_v[1].rearrange("p j n -> p (j n)")
        for run in (slice(0, 2 * N + 256), slice(3 * N, 3 * N + 256)):
            nc.sync.dma_start(out=flat_raw[:, run], in_=flat_x[:, run])
        nc.sync.dma_start(out=raw[1][:, 2:4, chunks[1]], in_=x_v[1][:, 2:4, chunks[1]])
        nc.sync.dma_start(out=w_sb[1][:].bitcast(I32), in_=w_v[1])

        for s in range(SETS):
            grouped = sb.tile([P, N, PACK], BF16, name="grouped%d" % s, align_bytes=64)
            codes = sb.tile([P, N], U32, name="codes%d" % s, align_bytes=64)
            scales = sb.tile([P, N], U8, name="scales%d" % s, align_bytes=64)
            if s == 0:
                shares = [(nc.scalar.copy, slice(320, 512)), (nc.vector.tensor_copy, slice(0, 256)), (nc.vector.tensor_copy, slice(256, 320))]
            else:
                shares = [(nc.vector.tensor_copy, cols) for cols in chunks]
            for cast, cols in shares:
                cast(
                    out=grouped[:, cols, :].rearrange("p (c i) j -> p c j i", i=4),
                    in_=raw[s][:, :, cols].rearrange("p j (c i) -> p c j i", i=4),
                )
            if s == 0:
                nc.vector.transpose(out=b_cols[:], in_=b_rows[:])
            for cols in chunks:
                nc.vector.quantize_mx(
                    out=codes[:, cols].bitcast(FP8X4),
                    scales=scales[:, cols],
                    in_=grouped[:, cols, :].rearrange("p n j -> p (n j)"),
                )
            for h in range(HALVES):
                for c in range(SIDE):
                    g = SIDE * s + c
                    k = HALVES * g + h
                    rows = slice(ROWS * c, ROWS * (c + 1))
                    acc = ps.tile([P, N], F32, name="acc%d" % k)
                    nc.tensor.matmul_mx(
                        out=acc[:],
                        lhsT=w_sb[s][rows, 2 * P * h : 2 * P * (h + 1)].bitcast(FP4X4),
                        lhsT_scale=ws_sb[rows, s, P * h : P * (h + 1)],
                        rhs=codes[rows, :].bitcast(FP8X4),
                        rhs_scale=scales[rows, :],
                        start=True,
                        stop=True,
                    )
                    res = sb.tile([P, N], F32, name="res%d" % k)
                    parts = chunks if h == 0 and c == 0 else [slice(0, N)]
                    for cols in parts:
                        nc.scalar.activation(
                            out=res[:, cols], in_=acc[:, cols], func=SILU, bias=b_cols[:, 4 * k : 4 * k + 1]
                        )
                        nc.sync.dma_start(out=out[g, P * h : P * (h + 1), cols], in_=res[:, cols])
